import numpy as np
CORES = [3,11,19,27,35,43,51,59,67,75,83,91]
N = 12
def setup_inputs(rng):
    return {"x": rng.standard_normal((N, 128, 256), dtype=np.float32)}
def reference(x):
    s = np.cumsum(x.astype(np.float64), axis=0)
    y = np.full(x.shape, np.nan, x.dtype)
    y[1:] = s[:-1]
    return {"y": y}

@@ -1,0 +1,87 @@
+from concourse.bass import DstId, RemoteDMATransfer
+
+N = 12
+NS = 32
+U = 256 // NS
+G = NS // 8
+RPG = 128 // G
+
+SCRATCH = {
+    "xs": ("dram", [NS, 128, U], "float32"),
+    "land": ("dram", [N - 1, 128, U], "float32"),
+    "res": ("dram", [NS, 128, U], "float32"),
+    "full": ("dram", [128, 256], "float32"),
+}
+SEMAPHORES = (["ld%d" % q for q in range(G)] + ["r%d" % q for q in range(G)]
+              + ["ldf", "arrf", "arr", "sent", "st"])
+
+CALL_A = {11: 0x03, 10: 0x0C, 9: 0x30, 8: 0xC0}
+CALL_B = {7: 0x03, 6: 0x0C, 5: 0x10, 4: 0x20, 3: 0x40, 2: 0x80}
+
+
+def owner_cores():
+    return [ch * 8 + k for k in (2, 6, 7) for ch in range(N)][:NS]
+
+
+def nbits(m):
+    return bin(m).count("1")
+
+
+def rank_program(g, core, T, topo):
+    rank = T.rank_of(core)
+    own = owner_cores()
+
+    def dst_id(c):
+        rid, pid, _se = topo.addr(c)
+        return DstId(rid=rid, pnc=pid)
+
+    if rank is not None:
+        queues = [g.sync, g.scalar]
+        sent = 0
+        if rank <= N - 2:
+            for q in range(G):
+                queues[q % 2].dma_start(T.xs[8 * q:8 * q + 8], T.x[RPG * q:RPG * (q + 1), :]).then_inc(
+                    T.sem["ld%d" % q], 16)
+            if rank == 0:
+                g.scalar.dma_start(T.full[:], T.x[:]).then_inc(T.sem.ldf, 16)
+            for q in range(G):
+                g.wait_ge(T.sem["ld%d" % q], 16)
+                g.remote_dma_fused(
+                    [RemoteDMATransfer(dst_ids=[dst_id(own[8 * q + t])], dma_engine_mask=1 << t,
+                                       remote_sem=T.sem.arr, src=T.xs[8 * q + t], dst=T.land[rank])
+                     for t in range(8)],
+                    local_sem=T.sem.sent)
+                sent += 8
+            if rank == 0:
+                rid, pid, _se = topo.addr(T.cores[1])
+                g.wait_ge(T.sem.ldf, 16)
+                g.remote_dma(T.full[:], T.full[:], T.sem.arrf, T.sem.sent, pid, rid, 0xFF)
+                sent += 8
+        stores = 0
+        if rank == 1:
+            g.sync.wait_ge(T.sem.arrf, 8)
+            g.sync.dma_start(T.y[:], T.full[:]).then_inc(T.sem.st, 16)
+            stores = 1
+        elif rank >= 2:
+            e = nbits(CALL_A[rank] if rank in CALL_A else CALL_B[rank])
+            for q in range(G):
+                queues[q % 2].wait_ge(T.sem["r%d" % q], 8 * e)
+                queues[q % 2].dma_start(T.y[RPG * q:RPG * (q + 1), :], T.res[8 * q:8 * q + 8]).then_inc(T.sem.st, 16)
+            stores = G
+        if stores:
+            g.wait_ge(T.sem.st, 16 * stores)
+        if sent:
+            g.wait_ge(T.sem.sent, sent)
+        return
+
+    if core in own:
+        s = own.index(core)
+        g.wait_ge(T.sem.arr, N - 1)
+        for call in (CALL_A, CALL_B):
+            g.remote_dma_fused(
+                [RemoteDMATransfer(dst_ids=[dst_id(T.cores[j])], dma_engine_mask=m,
+                                   remote_sem=T.sem["r%d" % (s // 8)],
+                                   srcs=[T.land[i] for i in range(j)], dsts=[T.res[s]], alu_op=1)
+                 for j, m in call.items()],
+                local_sem=T.sem.sent)
+        g.wait_ge(T.sem.sent, 16)

@@ -1,7 +1,7 @@
 from concourse.bass import DstId, RemoteDMATransfer
 
 N = 12
-NS = 32
+NS = 16
 U = 256 // NS
 G = NS // 8
 RPG = 128 // G
@@ -15,12 +15,17 @@ SCRATCH = {
 SEMAPHORES = (["ld%d" % q for q in range(G)] + ["r%d" % q for q in range(G)]
               + ["ldf", "arrf", "arr", "sent", "st"])
 
-CALL_A = {11: 0x03, 10: 0x0C, 9: 0x30, 8: 0xC0}
-CALL_B = {7: 0x03, 6: 0x0C, 5: 0x10, 4: 0x20, 3: 0x40, 2: 0x80}
+FOLDS = (
+    {10: 0x03, 8: 0x0C, 6: 0x30, 4: 0x40, 2: 0x80},
+    {11: 0x03, 9: 0x0C, 7: 0x30, 5: 0x40, 3: 0x80},
+)
 
 
-def owner_cores():
-    return [ch * 8 + k for k in (2, 6, 7) for ch in range(N)][:NS]
+def owner_cores(par):
+    chips = [c for c in range(N) if c % 2 == par]
+    slots = [c * 8 + 2 for c in chips] + [c * 8 + 6 for c in chips]
+    slots += [chips[0] * 8 + 1, chips[1] * 8 + 1, chips[2] * 8 + 5, chips[3] * 8 + 5]
+    return slots[:NS]
 
 
 def nbits(m):
@@ -29,7 +34,7 @@ def nbits(m):
 
 def rank_program(g, core, T, topo):
     rank = T.rank_of(core)
-    own = owner_cores()
+    own = (owner_cores(0), owner_cores(1))
 
     def dst_id(c):
         rid, pid, _se = topo.addr(c)
@@ -39,16 +44,18 @@ def rank_program(g, core, T, topo):
         queues = [g.sync, g.scalar]
         sent = 0
         if rank <= N - 2:
+            pars = [p for p in (0, 1) if rank < max(FOLDS[p])]
             for q in range(G):
                 queues[q % 2].dma_start(T.xs[8 * q:8 * q + 8], T.x[RPG * q:RPG * (q + 1), :]).then_inc(
                     T.sem["ld%d" % q], 16)
             if rank == 0:
-                g.scalar.dma_start(T.full[:], T.x[:]).then_inc(T.sem.ldf, 16)
+                g.sync.dma_start(T.full[:], T.x[:]).then_inc(T.sem.ldf, 16)
             for q in range(G):
                 g.wait_ge(T.sem["ld%d" % q], 16)
                 g.remote_dma_fused(
-                    [RemoteDMATransfer(dst_ids=[dst_id(own[8 * q + t])], dma_engine_mask=1 << t,
-                                       remote_sem=T.sem.arr, src=T.xs[8 * q + t], dst=T.land[rank])
+                    [RemoteDMATransfer(dst_ids=[dst_id(own[p][8 * q + t]) for p in pars], dma_engine_mask=1 << t,
+                                       remote_sem=T.sem.arr, srcs=[T.xs[8 * q + t]],
+                                       dsts=[T.land[rank] for p in pars])
                      for t in range(8)],
                     local_sem=T.sem.sent)
                 sent += 8
@@ -63,7 +70,7 @@ def rank_program(g, core, T, topo):
             g.sync.dma_start(T.y[:], T.full[:]).then_inc(T.sem.st, 16)
             stores = 1
         elif rank >= 2:
-            e = nbits(CALL_A[rank] if rank in CALL_A else CALL_B[rank])
+            e = nbits(FOLDS[rank % 2][rank])
             for q in range(G):
                 queues[q % 2].wait_ge(T.sem["r%d" % q], 8 * e)
                 queues[q % 2].dma_start(T.y[RPG * q:RPG * (q + 1), :], T.res[8 * q:8 * q + 8]).then_inc(T.sem.st, 16)
@@ -74,14 +81,15 @@ def rank_program(g, core, T, topo):
             g.wait_ge(T.sem.sent, sent)
         return
 
-    if core in own:
-        s = own.index(core)
-        g.wait_ge(T.sem.arr, N - 1)
-        for call in (CALL_A, CALL_B):
-            g.remote_dma_fused(
-                [RemoteDMATransfer(dst_ids=[dst_id(T.cores[j])], dma_engine_mask=m,
-                                   remote_sem=T.sem["r%d" % (s // 8)],
-                                   srcs=[T.land[i] for i in range(j)], dsts=[T.res[s]], alu_op=1)
-                 for j, m in call.items()],
-                local_sem=T.sem.sent)
-        g.wait_ge(T.sem.sent, 16)
+    par = topo.chip(core) % 2
+    if core in own[par]:
+        s = own[par].index(core)
+        folds = FOLDS[par]
+        g.wait_ge(T.sem.arr, max(folds))
+        g.remote_dma_fused(
+            [RemoteDMATransfer(dst_ids=[dst_id(T.cores[j])], dma_engine_mask=m,
+                               remote_sem=T.sem["r%d" % (s // 8)],
+                               srcs=[T.land[i] for i in range(j)], dsts=[T.res[s]], alu_op=1)
+             for j, m in folds.items()],
+            local_sem=T.sem.sent)
+        g.wait_ge(T.sem.sent, 8)

@@ -1,17 +1,15 @@
 from concourse.bass import DstId, RemoteDMATransfer
 
 N = 12
-NS = 16
-U = 256 // NS
-G = NS // 8
-RPG = 128 // G
+US = (15, 11, 6)
+G = len(US)
+ROW0 = [4 * sum(US[:q]) for q in range(G + 1)]
 
-SCRATCH = {
-    "xs": ("dram", [NS, 128, U], "float32"),
-    "land": ("dram", [N - 1, 128, U], "float32"),
-    "res": ("dram", [NS, 128, U], "float32"),
-    "full": ("dram", [128, 256], "float32"),
-}
+SCRATCH = {"full": ("dram", [128, 256], "float32")}
+for _q in range(G):
+    SCRATCH["xs%d" % _q] = ("dram", [8, 128, US[_q]], "float32")
+    SCRATCH["land%d" % _q] = ("dram", [N - 1, 128, US[_q]], "float32")
+    SCRATCH["res%d" % _q] = ("dram", [8, 128, US[_q]], "float32")
 SEMAPHORES = (["ld%d" % q for q in range(G)] + ["r%d" % q for q in range(G)]
               + ["ldf", "arrf", "arr", "sent", "st"])
 
@@ -23,9 +21,12 @@ FOLDS = (
 
 def owner_cores(par):
     chips = [c for c in range(N) if c % 2 == par]
-    slots = [c * 8 + 2 for c in chips] + [c * 8 + 6 for c in chips]
-    slots += [chips[0] * 8 + 1, chips[1] * 8 + 1, chips[2] * 8 + 5, chips[3] * 8 + 5]
-    return slots[:NS]
+    d1 = [c * 8 + k for k in (2, 1, 0) for c in chips]
+    d0 = [c * 8 + k for k in (6, 5, 4) for c in chips[3:] + chips[:3]]
+    out = []
+    for q in range(G):
+        out += d1[4 * q:4 * q + 4] + d0[4 * q:4 * q + 4]
+    return out
 
 
 def nbits(m):
@@ -46,16 +47,16 @@ def rank_program(g, core, T, topo):
         if rank <= N - 2:
             pars = [p for p in (0, 1) if rank < max(FOLDS[p])]
             for q in range(G):
-                queues[q % 2].dma_start(T.xs[8 * q:8 * q + 8], T.x[RPG * q:RPG * (q + 1), :]).then_inc(
+                queues[q % 2].dma_start(T["xs%d" % q][:], T.x[ROW0[q]:ROW0[q + 1], :]).then_inc(
                     T.sem["ld%d" % q], 16)
             if rank == 0:
-                g.sync.dma_start(T.full[:], T.x[:]).then_inc(T.sem.ldf, 16)
+                g.scalar.dma_start(T.full[:], T.x[:]).then_inc(T.sem.ldf, 16)
             for q in range(G):
                 g.wait_ge(T.sem["ld%d" % q], 16)
                 g.remote_dma_fused(
                     [RemoteDMATransfer(dst_ids=[dst_id(own[p][8 * q + t]) for p in pars], dma_engine_mask=1 << t,
-                                       remote_sem=T.sem.arr, srcs=[T.xs[8 * q + t]],
-                                       dsts=[T.land[rank] for p in pars])
+                                       remote_sem=T.sem.arr, srcs=[T["xs%d" % q][t]],
+                                       dsts=[T["land%d" % q][rank] for p in pars])
                      for t in range(8)],
                     local_sem=T.sem.sent)
                 sent += 8
@@ -73,7 +74,7 @@ def rank_program(g, core, T, topo):
             e = nbits(FOLDS[rank % 2][rank])
             for q in range(G):
                 queues[q % 2].wait_ge(T.sem["r%d" % q], 8 * e)
-                queues[q % 2].dma_start(T.y[RPG * q:RPG * (q + 1), :], T.res[8 * q:8 * q + 8]).then_inc(T.sem.st, 16)
+                queues[q % 2].dma_start(T.y[ROW0[q]:ROW0[q + 1], :], T["res%d" % q][:]).then_inc(T.sem.st, 16)
             stores = G
         if stores:
             g.wait_ge(T.sem.st, 16 * stores)
@@ -84,12 +85,13 @@ def rank_program(g, core, T, topo):
     par = topo.chip(core) % 2
     if core in own[par]:
         s = own[par].index(core)
+        q, t = s // 8, s % 8
         folds = FOLDS[par]
         g.wait_ge(T.sem.arr, max(folds))
         g.remote_dma_fused(
             [RemoteDMATransfer(dst_ids=[dst_id(T.cores[j])], dma_engine_mask=m,
-                               remote_sem=T.sem["r%d" % (s // 8)],
-                               srcs=[T.land[i] for i in range(j)], dsts=[T.res[s]], alu_op=1)
+                               remote_sem=T.sem["r%d" % q],
+                               srcs=[T["land%d" % q][i] for i in range(j)], dsts=[T["res%d" % q][t]], alu_op=1)
              for j, m in folds.items()],
             local_sem=T.sem.sent)
         g.wait_ge(T.sem.sent, 8)

from concourse.bass import DstId, RemoteDMATransfer

N = 12
US = (15, 11, 6)
G = len(US)
ROW0 = [4 * sum(US[:q]) for q in range(G + 1)]

SCRATCH = {"full": ("dram", [128, 256], "float32")}
for _q in range(G):
    SCRATCH["xs%d" % _q] = ("dram", [8, 128, US[_q]], "float32")
    SCRATCH["land%d" % _q] = ("dram", [N - 1, 128, US[_q]], "float32")
    SCRATCH["res%d" % _q] = ("dram", [8, 128, US[_q]], "float32")
SEMAPHORES = (["ld%d" % q for q in range(G)] + ["r%d" % q for q in range(G)]
              + ["ldf", "arrf", "arr", "sent", "st"])

FOLDS = (
    {10: 0x03, 8: 0x0C, 6: 0x30, 4: 0x40, 2: 0x80},
    {11: 0x03, 9: 0x0C, 7: 0x30, 5: 0x40, 3: 0x80},
)


def owner_cores(par):
    chips = [c for c in range(N) if c % 2 == par]
    d1 = [c * 8 + k for k in (2, 1, 0) for c in chips]
    d0 = [c * 8 + k for k in (6, 5, 4) for c in chips[3:] + chips[:3]]
    out = []
    for q in range(G):
        out += d1[4 * q:4 * q + 4] + d0[4 * q:4 * q + 4]
    return out


def nbits(m):
    return bin(m).count("1")


def rank_program(g, core, T, topo):
    rank = T.rank_of(core)
    own = (owner_cores(0), owner_cores(1))

    def dst_id(c):
        rid, pid, _se = topo.addr(c)
        return DstId(rid=rid, pnc=pid)

    if rank is not None:
        queues = [g.sync, g.scalar]
        sent = 0
        if rank <= N - 2:
            pars = [p for p in (0, 1) if rank < max(FOLDS[p])]
            for q in range(G):
                queues[q % 2].dma_start(T["xs%d" % q][:], T.x[ROW0[q]:ROW0[q + 1], :]).then_inc(
                    T.sem["ld%d" % q], 16)
            if rank == 0:
                g.scalar.dma_start(T.full[:], T.x[:]).then_inc(T.sem.ldf, 16)
            for q in range(G):
                g.wait_ge(T.sem["ld%d" % q], 16)
                g.remote_dma_fused(
                    [RemoteDMATransfer(dst_ids=[dst_id(own[p][8 * q + t]) for p in pars], dma_engine_mask=1 << t,
                                       remote_sem=T.sem.arr, srcs=[T["xs%d" % q][t]],
                                       dsts=[T["land%d" % q][rank] for p in pars])
                     for t in range(8)],
                    local_sem=T.sem.sent)
                sent += 8
            if rank == 0:
                rid, pid, _se = topo.addr(T.cores[1])
                g.wait_ge(T.sem.ldf, 16)
                g.remote_dma(T.full[:], T.full[:], T.sem.arrf, T.sem.sent, pid, rid, 0xFF)
                sent += 8
        stores = 0
        if rank == 1:
            g.sync.wait_ge(T.sem.arrf, 8)
            g.sync.dma_start(T.y[:], T.full[:]).then_inc(T.sem.st, 16)
            stores = 1
        elif rank >= 2:
            e = nbits(FOLDS[rank % 2][rank])
            for q in range(G):
                queues[q % 2].wait_ge(T.sem["r%d" % q], 8 * e)
                queues[q % 2].dma_start(T.y[ROW0[q]:ROW0[q + 1], :], T["res%d" % q][:]).then_inc(T.sem.st, 16)
            stores = G
        if stores:
            g.wait_ge(T.sem.st, 16 * stores)
        if sent:
            g.wait_ge(T.sem.sent, sent)
        return

    par = topo.chip(core) % 2
    if core in own[par]:
        s = own[par].index(core)
        q, t = s // 8, s % 8
        folds = FOLDS[par]
        g.wait_ge(T.sem.arr, max(folds))
        g.remote_dma_fused(
            [RemoteDMATransfer(dst_ids=[dst_id(T.cores[j])], dma_engine_mask=m,
                               remote_sem=T.sem["r%d" % q],
                               srcs=[T["land%d" % q][i] for i in range(j)], dsts=[T["res%d" % q][t]], alu_op=1)
             for j, m in folds.items()],
            local_sem=T.sem.sent)
        g.wait_ge(T.sem.sent, 8)
